import numpy as np
import ml_dtypes


def mxq(x, axis, fmt="e4m3"):
    dtype, down = {"e4m3": (ml_dtypes.float8_e4m3fn, 7), "e5m2": (ml_dtypes.float8_e5m2, 14)}[fmt]
    v = np.moveaxis(np.asarray(x, np.float32).astype(ml_dtypes.bfloat16).astype(np.float64), axis, -1)
    blocks = v.reshape(v.shape[:-1] + (-1, 32))
    amax = np.abs(blocks).max(-1, keepdims=True)
    byte = np.maximum(np.where(amax > 0, np.frexp(amax)[1] - 1 + 127, 0) - down, 1)
    scale = np.exp2(byte - 127.0)
    codes = (blocks / scale).astype(np.float32).astype(dtype).astype(np.float64)
    return np.moveaxis((codes * scale).reshape(v.shape), -1, axis)


WIDE = False


def mx_kscale(k):
    if not WIDE:
        return np.ones(k)
    levels = np.array([10, -10, 5, -5, 0])
    if k % 512:
        return np.exp2(np.random.permutation(np.resize(levels, k // 32))).repeat(32)
    a = np.empty((k // 512, 16))
    for p in range(k // 512):
        a[p, :8] = np.random.permutation(np.resize(levels, 8))
        for g in range(8):
            far = levels[np.abs(levels - a[p, g]) >= 10]
            a[p, g + 8] = far[np.random.randint(len(far))]
    return np.exp2(a.ravel()).repeat(32)


def f64(x):
    return np.asarray(x).astype(np.float64)


def striped(idx):
    return np.tile(idx.reshape(-1, 16).T, (8, 1)).astype(np.uint16)


def unstriped(offs):
    return offs[:16].T.reshape(-1).astype(np.int64)


E2M1 = np.array([0.0, 0.5, 1.0, 1.5, 2.0, 3.0, 4.0, 6.0, -0.0, -0.5, -1.0, -1.5, -2.0, -3.0, -4.0, -6.0])


def pack_weight(w, fmt):
    k, n = w.shape
    w = f64(np.asarray(w, np.float32).astype(ml_dtypes.bfloat16)).reshape(k // 32, 32, n)
    amax = np.abs(w).max(1)
    if fmt == "e4m3":
        byte = np.frexp(amax)[1] - 1 + 127 - 7
    else:
        mant, ex = np.frexp(amax / 6.0)
        byte = np.where(mant > 0.5, ex, ex - 1) + 127
    byte = np.clip(np.where(amax > 0, byte, 1), 1, 254)
    scaled = (w * np.exp2(127.0 - byte)[:, None, :]).reshape(k, n).astype(np.float32)
    by_word = np.ascontiguousarray(scaled.reshape(k // 512, 128, 4, n).transpose(0, 1, 3, 2))
    if fmt == "e4m3":
        words = by_word.astype(ml_dtypes.float8_e4m3fn).view(np.uint8)
    else:
        c = by_word.astype(ml_dtypes.float4_e2m1fn).view(np.uint8) & 0xF
        words = (c[..., 0::2] | (c[..., 1::2] << 4)).reshape(k // 512, 128, 2 * n)
    return np.ascontiguousarray(words), np.ascontiguousarray(byte.astype(np.uint8).reshape(k // 512, 16, n))


def unpack_weight(words, scales, fmt):
    g, _, n = scales.shape
    words = np.ascontiguousarray(words).reshape(g, 128, n, -1)
    if fmt == "e4m3":
        vals = words.view(ml_dtypes.float8_e4m3fn).astype(np.float64)
    else:
        nib = np.empty((g, 128, n, 4), np.uint8)
        nib[..., 0::2] = words & 0xF
        nib[..., 1::2] = words >> 4
        vals = E2M1[nib]
    vals = vals * np.repeat(np.exp2(scales.astype(np.float64) - 127.0), 8, axis=1)[..., None]
    return vals.transpose(0, 1, 3, 2).reshape(g * 512, n)


K, T, E, C, N = 1024, 512, 8, 256, 256
TOP = 4


def by_expert(wq, xq):
    return np.concatenate([wq[e].T @ xq[:, e * C:(e + 1) * C] for e in range(E)], axis=1)


def setup_inputs():
    n = np.random.standard_normal
    s = mx_kscale(K)[:, None]
    deal = np.repeat(np.arange(E), C).reshape(TOP, T)[:, np.random.permutation(T)]
    deal = np.take_along_axis(deal, np.argsort(np.random.rand(TOP, T), axis=0), axis=0)
    for _ in range(8):
        s_, t_ = np.random.permutation(T).reshape(2, -1); r = np.random.randint(TOP, size=T // 2); x, y = deal[r, s_].copy(), deal[r, t_].copy()
        ok = ~((deal[:, s_] == y).any(0) | (deal[:, t_] == x).any(0)); deal[r[ok], s_[ok]] = y[ok]; deal[r[ok], t_[ok]] = x[ok]
    order = np.lexsort((np.random.rand(TOP * T), deal.reshape(-1)))
    slot_token = order % T; pos = np.empty(TOP * T, np.int64); pos[order] = np.arange(TOP * T); pos = pos.reshape(TOP, T)
    g = np.random.uniform(0.5, 1.5, (TOP, T)); g = g / g.sum(0)
    w = [pack_weight(m, "e2m1") for m in n((E, K, N)) / np.sqrt(K) / s[None]]
    w_slot = np.empty(E * C)
    for r in range(TOP): w_slot[pos[r]] = g[r]
    return {
        "xT": (n((K, T)) * s).astype(np.float32),
        "w_words": np.stack([m[0] for m in w]),
        "w_scales": np.stack([m[1] for m in w]),
        "gate": np.tile(w_slot, (K, 1)).astype(np.float32),
        "offs": striped(slot_token),
        "pos1": striped(pos[0]),
        "pos2": striped(pos[1]),
        "pos3": striped(pos[2]),
        "pos4": striped(pos[3]),
    }


def reference(xT, w_words, w_scales, gate, offs, pos1, pos2, pos3, pos4):
    idx = unstriped(offs)
    w = np.stack([unpack_weight(w_words[e], w_scales[e], "e2m1") for e in range(E)])
    xq = mxq(f64(gate) * f64(xT)[:, idx], 0, "e4m3")
    y = by_expert(w, xq)
    return y[:, unstriped(pos1)] + y[:, unstriped(pos2)] + y[:, unstriped(pos3)] + y[:, unstriped(pos4)]

@@ -1,0 +1,246 @@
+from contextlib import ExitStack
+
+import concourse.mybir as mybir
+
+K, T, E, C, N = 1024, 512, 8, 256, 256
+SLOTS = E * C
+FLOPS = 2 * K * SLOTS * N
+BYTES = 4 * K * T + E * K * N // 2 + E * K * N // 32 + 4 * SLOTS + 2 * 128 * 256 + 4 * N * T
+
+F32 = mybir.dt.float32
+BF16 = mybir.dt.bfloat16
+I32 = mybir.dt.int32
+U32 = mybir.dt.uint32
+U16 = mybir.dt.uint16
+U8 = mybir.dt.uint8
+FP8X4 = mybir.dt.float8_e4m3fn_x4
+FP4X4 = mybir.dt.float4_e2m1fn_x4
+MULT = mybir.AluOpType.mult
+ADD = mybir.AluOpType.add
+COPY = mybir.ActivationFunctionType.Copy
+
+P = 128
+PACK = 4
+PASSES = 2
+HALVES = 2
+RUN = 4
+LIST_COLS = C // 16
+PAIR = 2 * C
+WINDOW = T + 32
+OWN = 192
+
+
+def tile_moe_pre_lin_none_kernel(
+    tc, xT, w_words, w_scales, gate, offs, pos1, pos2, pos3, pos4, out
+):
+    nc = tc.nc
+    with ExitStack() as ctx:
+        keep = ctx.enter_context(tc.tile_pool(name="keep", bufs=1))
+        sg_pool = ctx.enter_context(tc.tile_pool(name="sg", bufs=6))
+        vg_pool = ctx.enter_context(tc.tile_pool(name="vg", bufs=1))
+        xb_pool = ctx.enter_context(tc.tile_pool(name="xb", bufs=3))
+        psum = ctx.enter_context(tc.psum_pool(name="psum", bufs=1))
+
+        w_plane = keep.tile([P, E * PASSES, N], U8, align_bytes=64)
+        nc.vector.memset(w_plane[:].rearrange("p g n -> p (g n)").bitcast(I32), 0)
+
+        offs_sb = keep.tile([P, SLOTS // 16], U16)
+        nc.sync.dma_start(offs_sb[:], offs)
+        x_rows = xT.rearrange("(a p t) w -> a t p w", a=PASSES, t=PACK)
+        x_sb = {}
+        gate_sb = {}
+
+        def load_x(a, t):
+            x_sb[a, t] = keep.tile([P, WINDOW], F32, name="x%d%d" % (a, t))
+            nc.gpsimd.memset(x_sb[a, t][:, T:WINDOW], 0.0)
+            nc.sync.dma_start(x_sb[a, t][:, 0:T], x_rows[a, t])
+
+        def load_gate(d):
+            gate_sb[d] = keep.tile([P, PAIR], F32, name="gate%d" % d)
+            nc.sync.dma_start(gate_sb[d][:], gate[0:P, d * PAIR : (d + 1) * PAIR])
+
+        load_x(0, 0)
+        load_gate(0)
+        for t in range(1, PACK):
+            load_x(0, t)
+        load_gate(1)
+        load_gate(2)
+        for t in range(PACK):
+            load_x(1, t)
+        load_gate(3)
+        w_rows = w_words.rearrange("e a p b -> p (e a) b").bitcast(I32)
+        w_sb = keep.tile([P, E * PASSES, 2 * N], U8, align_bytes=64)
+        for g0 in range(0, E * PASSES, E):
+            nc.sync.dma_start(w_sb[:, g0 : g0 + E, :].bitcast(I32), w_rows[:, g0 : g0 + E, :])
+        scale_rows = w_scales.rearrange("e a (q r) n -> r q (e a) n", r=4).bitcast(I32)
+        for r in range(4):
+            nc.sync.dma_start(w_plane[r:P:32, :, :].bitcast(I32), scale_rows[r])
+        pos_sb = []
+        for r, pos in enumerate((pos1, pos2, pos3, pos4)):
+            pos_sb.append(keep.tile([P, T // 16], U16, name="pos%d" % r))
+            nc.sync.dma_start(pos_sb[r][:], pos)
+
+        def slots_of(d, a, t):
+            cols = PAIR // 16
+            return x_sb[a, t][:].indirect(offs_sb[:, d * cols : (d + 1) * cols])
+
+        def by_runs(planes):
+            return planes.rearrange("p t (c i) -> p c t i", i=RUN)
+
+        def woven(xb):
+            return xb.rearrange("p (c i) t -> p c t i", i=RUN)
+
+        codes = {}
+        scales = {}
+
+        def quantize(e, count, a, xb):
+            words = keep.tile([P, count * C], U32, name="codes%d%d" % (e, a), align_bytes=64)
+            plane = keep.tile([P, count * C], U8, name="scales%d%d" % (e, a), align_bytes=64)
+            nc.vector.quantize_mx(
+                out=words[:].bitcast(FP8X4),
+                scales=plane[:],
+                in_=xb[:].rearrange("p c t -> p (c t)"),
+            )
+            for m in range(count):
+                codes[e + m, a] = words[:, m * C : (m + 1) * C]
+                scales[e + m, a] = plane[:, m * C : (m + 1) * C]
+
+        s_steps = [(1, 0), (2, 0), (1, 1), (2, 1), (3, 0), (3, 1)]
+
+        s_planes = []
+        for d, a in s_steps:
+            planes = sg_pool.tile([P, PACK, PAIR], F32, name="s_planes")
+            for t in range(PACK):
+                nc.scalar.activation(planes[:, t, :], slots_of(d, a, t), COPY)
+            s_planes.append(planes)
+
+        v_planes = {}
+
+        def v_gather(a, t):
+            if t == 0:
+                v_planes[a] = vg_pool.tile([P, PACK, PAIR], F32, name="v_planes")
+            nc.vector.tensor_tensor(v_planes[a][:, t, :], slots_of(0, a, t), gate_sb[0][:], MULT)
+
+        def v_weave(a):
+            xz = xb_pool.tile([P, PAIR, PACK], BF16, name="xb", align_bytes=64)
+            nc.vector.tensor_copy(woven(xz[:]), by_runs(v_planes[a][:]))
+            return xz
+
+        def gate_weave(i, c0, width):
+            d = s_steps[i][0]
+            xb = xb_pool.tile([P, width, PACK], BF16, name="xb", align_bytes=64)
+            g = gate_sb[d][:, c0 : c0 + width].rearrange("p (c i) -> p c i", i=RUN)
+            g = g.unsqueeze(2).to_broadcast([P, width // RUN, PACK, RUN])
+            nc.vector.tensor_tensor(woven(xb[:]), by_runs(s_planes[i][:, :, c0 : c0 + width]), g, MULT)
+            return xb
+
+        def one_pass(bank, e, h, a):
+            g = e * PASSES + a
+            nc.tensor.matmul_mx(
+                out=bank,
+                lhsT=w_sb[:, g, 2 * P * h : 2 * P * (h + 1)].bitcast(FP4X4),
+                lhsT_scale=w_plane[:, g, P * h : P * (h + 1)],
+                rhs=codes[e, a].bitcast(FP8X4),
+                rhs_scale=scales[e, a],
+                start=(a == 0),
+                stop=(a == PASSES - 1),
+            )
+
+        banks = {}
+
+        def multiply_pair(d):
+            for h in range(HALVES):
+                banks[d, h] = psum.tile([P, PAIR], F32, name="bank%d%d" % (d, h))
+                for m in range(2):
+                    for a in range(PASSES):
+                        one_pass(banks[d, h][:, m * C : (m + 1) * C], 2 * d + m, h, a)
+
+        y_sb = [keep.tile([P, SLOTS], F32, name="y%d" % h) for h in range(HALVES)]
+
+        def empty_pair(d):
+            for h in range(HALVES):
+                nc.scalar.copy(y_sb[h][:, d * PAIR : (d + 1) * PAIR], banks[d, h][:])
+
+        for t in range(PACK):
+            v_gather(0, t)
+        xb = gate_weave(0, 0, PAIR)
+        xz = v_weave(0)
+        quantize(2, 2, 0, xb)
+        quantize(0, 2, 0, xz)
+        xb = gate_weave(1, 0, PAIR)
+        v_gather(1, 0)
+        quantize(4, 2, 0, xb)
+        v_gather(1, 1)
+        xb = gate_weave(2, 0, PAIR)
+        v_gather(1, 2)
+        quantize(2, 2, 1, xb)
+        multiply_pair(1)
+        xb = gate_weave(3, 0, PAIR)
+        v_gather(1, 3)
+        quantize(4, 2, 1, xb)
+        multiply_pair(2)
+        xb = gate_weave(4, 0, PAIR)
+        xz = v_weave(1)
+        quantize(6, 2, 0, xb)
+        quantize(0, 2, 1, xz)
+        multiply_pair(0)
+        xb6 = gate_weave(5, 0, C)
+        xb7 = gate_weave(5, C, C)
+        quantize(6, 1, 1, xb6)
+        quantize(7, 1, 1, xb7)
+        empty_pair(1)
+        last = {}
+        for h in range(HALVES):
+            last[6, h] = psum.tile([P, C], F32, name="bank3%d" % h)
+            last[7, h] = psum.tile([P, C], F32, name="bank1%d" % h)
+        for a in range(PASSES):
+            for e in (6, 7):
+                for h in range(HALVES):
+                    one_pass(last[e, h][:], e, h, a)
+        empty_pair(2)
+        empty_pair(0)
+        for e in (6, 7):
+            nc.scalar.copy(y_sb[0][:, e * C : (e + 1) * C], last[e, 0][:])
+            nc.vector.tensor_copy(y_sb[1][:, e * C : (e + 1) * C], last[e, 1][:])
+
+        def picked(h, t0, t1, r):
+            return y_sb[h][:].indirect(pos_sb[r][:, t0 // 16 : t1 // 16])
+
+        def store(h, t0, t1, tile):
+            nc.sync.dma_start(out[h * P : (h + 1) * P, t0:t1], tile[:])
+
+        shared = [(0, 0, T), (1, OWN, T)]
+        fetched = []
+        for m, (h, t0, t1) in enumerate(shared):
+            three = [keep.tile([P, t1 - t0], F32, name="f%d%d" % (m, r)) for r in range(3)]
+            for r in range(3):
+                nc.scalar.activation(three[r][:], picked(h, t0, t1, r), COPY)
+            fetched.append(three)
+
+        own = [keep.tile([P, OWN], F32, name="own%d" % r) for r in range(4)]
+        acc = [[keep.tile([P, t1 - t0], F32, name="acc%d%d" % (h, r)) for r in range(3)] for h, t0, t1 in shared]
+
+        def own_step(r):
+            if r == 0:
+                nc.vector.tensor_copy(own[0][:], picked(1, 0, OWN, 0))
+            else:
+                nc.vector.tensor_tensor(own[r][:], picked(1, 0, OWN, r), own[r - 1][:], ADD)
+
+        def shared_step(m, r):
+            if r == 0:
+                nc.vector.tensor_tensor(acc[m][0][:], picked(*shared[m], 3), fetched[m][0][:], ADD)
+            else:
+                nc.vector.tensor_tensor(acc[m][r][:], acc[m][r - 1][:], fetched[m][r][:], ADD)
+
+        own_step(0)
+        own_step(1)
+        shared_step(0, 0)
+        own_step(2)
+        shared_step(0, 1)
+        own_step(3)
+        store(1, 0, OWN, own[3])
+        shared_step(0, 2)
+        store(*shared[0], acc[0][2])
+        for r in range(3):
+            shared_step(1, r)
+        store(*shared[1], acc[1][2])

@@ -26,8 +26,10 @@ HALVES = 2
 RUN = 4
 LIST_COLS = C // 16
 PAIR = 2 * C
-WINDOW = T + 32
-OWN = 192
+WINDOW = 2 * T
+OWN = 128
+EXTRA = 32
+V_SLOTS = PAIR + EXTRA
 
 
 def tile_moe_pre_lin_none_kernel(
@@ -36,38 +38,38 @@ def tile_moe_pre_lin_none_kernel(
     nc = tc.nc
     with ExitStack() as ctx:
         keep = ctx.enter_context(tc.tile_pool(name="keep", bufs=1))
-        sg_pool = ctx.enter_context(tc.tile_pool(name="sg", bufs=6))
-        vg_pool = ctx.enter_context(tc.tile_pool(name="vg", bufs=1))
         xb_pool = ctx.enter_context(tc.tile_pool(name="xb", bufs=3))
         psum = ctx.enter_context(tc.psum_pool(name="psum", bufs=1))
 
+        x_sb = {}
+        for a in range(PASSES):
+            for t in range(PACK):
+                x_sb[a, t] = keep.tile([P, WINDOW], F32, name="x%d%d" % (a, t))
+                if (a, t) != (0, 0):
+                    (nc.vector, nc.gpsimd)[a].memset(x_sb[a, t][:, T:WINDOW], 0.0)
+        nc.scalar.activation(x_sb[0, 0][:, T:WINDOW], x_sb[0, 1][:, T:WINDOW], COPY)
         w_plane = keep.tile([P, E * PASSES, N], U8, align_bytes=64)
-        nc.vector.memset(w_plane[:].rearrange("p g n -> p (g n)").bitcast(I32), 0)
+        nc.gpsimd.memset(w_plane[:].rearrange("p g n -> p (g n)").bitcast(I32), 0)
 
         offs_sb = keep.tile([P, SLOTS // 16], U16)
         nc.sync.dma_start(offs_sb[:], offs)
         x_rows = xT.rearrange("(a p t) w -> a t p w", a=PASSES, t=PACK)
-        x_sb = {}
-        gate_sb = {}
 
         def load_x(a, t):
-            x_sb[a, t] = keep.tile([P, WINDOW], F32, name="x%d%d" % (a, t))
-            nc.gpsimd.memset(x_sb[a, t][:, T:WINDOW], 0.0)
             nc.sync.dma_start(x_sb[a, t][:, 0:T], x_rows[a, t])
 
-        def load_gate(d):
-            gate_sb[d] = keep.tile([P, PAIR], F32, name="gate%d" % d)
-            nc.sync.dma_start(gate_sb[d][:], gate[0:P, d * PAIR : (d + 1) * PAIR])
+        def load_gate(name, s0, s1):
+            tile = keep.tile([P, s1 - s0], F32, name=name, align_bytes=64)
+            nc.sync.dma_start(tile[:], gate[0:P, s0:s1])
+            return tile
 
         load_x(0, 0)
-        load_gate(0)
+        gate_v = load_gate("gate_v", 0, V_SLOTS)
         for t in range(1, PACK):
             load_x(0, t)
-        load_gate(1)
-        load_gate(2)
         for t in range(PACK):
             load_x(1, t)
-        load_gate(3)
+        gate_s = load_gate("gate_s", V_SLOTS, SLOTS)
         w_rows = w_words.rearrange("e a p b -> p (e a) b").bitcast(I32)
         w_sb = keep.tile([P, E * PASSES, 2 * N], U8, align_bytes=64)
         for g0 in range(0, E * PASSES, E):
@@ -80,9 +82,8 @@ def tile_moe_pre_lin_none_kernel(
             pos_sb.append(keep.tile([P, T // 16], U16, name="pos%d" % r))
             nc.sync.dma_start(pos_sb[r][:], pos)
 
-        def slots_of(d, a, t):
-            cols = PAIR // 16
-            return x_sb[a, t][:].indirect(offs_sb[:, d * cols : (d + 1) * cols])
+        def slots_of(s0, s1, a, t):
+            return x_sb[a, t][:].indirect(offs_sb[:, s0 // 16 : s1 // 16])
 
         def by_runs(planes):
             return planes.rearrange("p t (c i) -> p c t i", i=RUN)
@@ -105,34 +106,29 @@ def tile_moe_pre_lin_none_kernel(
                 codes[e + m, a] = words[:, m * C : (m + 1) * C]
                 scales[e + m, a] = plane[:, m * C : (m + 1) * C]
 
-        s_steps = [(1, 0), (2, 0), (1, 1), (2, 1), (3, 0), (3, 1)]
-
-        s_planes = []
-        for d, a in s_steps:
-            planes = sg_pool.tile([P, PACK, PAIR], F32, name="s_planes")
+        def s_gather(s0, s1, a, name):
+            planes = keep.tile([P, PACK, s1 - s0], F32, name=name)
             for t in range(PACK):
-                nc.scalar.activation(planes[:, t, :], slots_of(d, a, t), COPY)
-            s_planes.append(planes)
+                nc.scalar.activation(planes[:, t, :], slots_of(s0, s1, a, t), COPY)
+            return planes
 
         v_planes = {}
 
         def v_gather(a, t):
             if t == 0:
-                v_planes[a] = vg_pool.tile([P, PACK, PAIR], F32, name="v_planes")
-            nc.vector.tensor_tensor(v_planes[a][:, t, :], slots_of(0, a, t), gate_sb[0][:], MULT)
+                v_planes[a] = keep.tile([P, PACK, V_SLOTS], F32, name="v_planes%d" % a)
+            nc.vector.tensor_tensor(v_planes[a][:, t, :], slots_of(0, V_SLOTS, a, t), gate_v[:], MULT)
 
-        def v_weave(a):
-            xz = xb_pool.tile([P, PAIR, PACK], BF16, name="xb", align_bytes=64)
-            nc.vector.tensor_copy(woven(xz[:]), by_runs(v_planes[a][:]))
-            return xz
+        def weave(dst, planes):
+            nc.vector.tensor_copy(woven(dst), by_runs(planes))
 
-        def gate_weave(i, c0, width):
-            d = s_steps[i][0]
-            xb = xb_pool.tile([P, width, PACK], BF16, name="xb", align_bytes=64)
-            g = gate_sb[d][:, c0 : c0 + width].rearrange("p (c i) -> p c i", i=RUN)
-            g = g.unsqueeze(2).to_broadcast([P, width // RUN, PACK, RUN])
-            nc.vector.tensor_tensor(woven(xb[:]), by_runs(s_planes[i][:, :, c0 : c0 + width]), g, MULT)
-            return xb
+        def gate_weave(dst, planes, p0, s0, s1):
+            g = gate_s[:, s0 - V_SLOTS : s1 - V_SLOTS].rearrange("p (c i) -> p c i", i=RUN)
+            g = g.unsqueeze(2).to_broadcast([P, (s1 - s0) // RUN, PACK, RUN])
+            nc.vector.tensor_tensor(woven(dst), by_runs(planes[:, :, s0 - p0 : s1 - p0]), g, MULT)
+
+        def bf16_tile(width):
+            return xb_pool.tile([P, width, PACK], BF16, name="xb", align_bytes=64)
 
         def one_pass(bank, e, h, a):
             g = e * PASSES + a
@@ -155,50 +151,63 @@ def tile_moe_pre_lin_none_kernel(
                     for a in range(PASSES):
                         one_pass(banks[d, h][:, m * C : (m + 1) * C], 2 * d + m, h, a)
 
-        y_sb = [keep.tile([P, SLOTS], F32, name="y%d" % h) for h in range(HALVES)]
 
-        def empty_pair(d):
-            for h in range(HALVES):
-                nc.scalar.copy(y_sb[h][:, d * PAIR : (d + 1) * PAIR], banks[d, h][:])
+        def empty(d, h, copy):
+            copy(y_sb[h][:, d * PAIR : (d + 1) * PAIR], banks[d, h][:])
 
+        mid = [s_gather(V_SLOTS, 3 * PAIR, a, "mid%d" % a) for a in range(PASSES)]
+        x1 = [keep.tile([P, PAIR, PACK], BF16, name="x1_%d" % a, align_bytes=64) for a in range(PASSES)]
         for t in range(PACK):
             v_gather(0, t)
-        xb = gate_weave(0, 0, PAIR)
-        xz = v_weave(0)
-        quantize(2, 2, 0, xb)
-        quantize(0, 2, 0, xz)
-        xb = gate_weave(1, 0, PAIR)
+        xz = bf16_tile(PAIR)
+        weave(xz[:], v_planes[0][:, :, 0:PAIR])
+        weave(x1[0][:, 0:EXTRA, :], v_planes[0][:, :, PAIR:V_SLOTS])
+        end = [s_gather(3 * PAIR, SLOTS, 0, "v_planes0"), s_gather(3 * PAIR, SLOTS, 1, "end1")]
         v_gather(1, 0)
-        quantize(4, 2, 0, xb)
-        v_gather(1, 1)
-        xb = gate_weave(2, 0, PAIR)
-        v_gather(1, 2)
-        quantize(2, 2, 1, xb)
-        multiply_pair(1)
-        xb = gate_weave(3, 0, PAIR)
-        v_gather(1, 3)
-        quantize(4, 2, 1, xb)
-        multiply_pair(2)
-        xb = gate_weave(4, 0, PAIR)
-        xz = v_weave(1)
-        quantize(6, 2, 0, xb)
+        quantize(0, 2, 0, xz)
+        for t in range(1, PACK):
+            v_gather(1, t)
+        xb20 = keep.tile([P, PAIR, PACK], BF16, name="gate_v", align_bytes=64)
+        gate_weave(xb20[:], mid[0], V_SLOTS, 2 * PAIR, 3 * PAIR)
+        xz = bf16_tile(PAIR)
+        weave(xz[:], v_planes[1][:, :, 0:PAIR])
+        weave(x1[1][:, 0:EXTRA, :], v_planes[1][:, :, PAIR:V_SLOTS])
+        quantize(4, 2, 0, xb20)
+        gate_weave(x1[0][:, EXTRA:PAIR, :], mid[0], V_SLOTS, V_SLOTS, 2 * PAIR)
         quantize(0, 2, 1, xz)
         multiply_pair(0)
-        xb6 = gate_weave(5, 0, C)
-        xb7 = gate_weave(5, C, C)
+        gate_weave(x1[1][:, EXTRA:PAIR, :], mid[1], V_SLOTS, V_SLOTS, 2 * PAIR)
+        quantize(2, 2, 0, x1[0])
+        xb21 = bf16_tile(PAIR)
+        gate_weave(xb21[:], mid[1], V_SLOTS, 2 * PAIR, 3 * PAIR)
+        quantize(2, 2, 1, x1[1])
+        multiply_pair(1)
+        xb30 = bf16_tile(PAIR)
+        gate_weave(xb30[:], end[0], 3 * PAIR, 3 * PAIR, SLOTS)
+        quantize(4, 2, 1, xb21)
+        multiply_pair(2)
+        quantize(6, 2, 0, xb30)
+        xb6 = bf16_tile(C)
+        gate_weave(xb6[:], end[1], 3 * PAIR, 6 * C, 7 * C)
+        xb7 = bf16_tile(C)
+        gate_weave(xb7[:], end[1], 3 * PAIR, 7 * C, 8 * C)
         quantize(6, 1, 1, xb6)
         quantize(7, 1, 1, xb7)
-        empty_pair(1)
+        y_sb = [keep.tile([P, SLOTS], F32, name="y%d" % h) for h in range(HALVES)]
+        for h in range(HALVES):
+            empty(0, h, nc.scalar.copy)
         last = {}
         for h in range(HALVES):
             last[6, h] = psum.tile([P, C], F32, name="bank3%d" % h)
-            last[7, h] = psum.tile([P, C], F32, name="bank1%d" % h)
+            last[7, h] = psum.tile([P, C], F32, name="bank0%d" % h)
         for a in range(PASSES):
             for e in (6, 7):
                 for h in range(HALVES):
                     one_pass(last[e, h][:], e, h, a)
-        empty_pair(2)
-        empty_pair(0)
+        empty(1, 0, nc.scalar.copy)
+        empty(2, 0, nc.scalar.copy)
+        empty(1, 1, nc.scalar.copy)
+        empty(2, 1, nc.vector.tensor_copy)
         for e in (6, 7):
             nc.scalar.copy(y_sb[0][:, e * C : (e + 1) * C], last[e, 0][:])
             nc.vector.tensor_copy(y_sb[1][:, e * C : (e + 1) * C], last[e, 1][:])
@@ -218,7 +227,7 @@ def tile_moe_pre_lin_none_kernel(
             fetched.append(three)
 
         own = [keep.tile([P, OWN], F32, name="own%d" % r) for r in range(4)]
-        acc = [[keep.tile([P, t1 - t0], F32, name="acc%d%d" % (h, r)) for r in range(3)] for h, t0, t1 in shared]
+        acc = {}
 
         def own_step(r):
             if r == 0:
@@ -227,20 +236,23 @@ def tile_moe_pre_lin_none_kernel(
                 nc.vector.tensor_tensor(own[r][:], picked(1, 0, OWN, r), own[r - 1][:], ADD)
 
         def shared_step(m, r):
+            h, t0, t1 = shared[m]
+            acc[m, r] = keep.tile([P, t1 - t0], F32, name="acc%d%d" % (m, r))
             if r == 0:
-                nc.vector.tensor_tensor(acc[m][0][:], picked(*shared[m], 3), fetched[m][0][:], ADD)
+                nc.vector.tensor_tensor(acc[m, 0][:], picked(h, t0, t1, 3), fetched[m][0][:], ADD)
             else:
-                nc.vector.tensor_tensor(acc[m][r][:], acc[m][r - 1][:], fetched[m][r][:], ADD)
+                nc.vector.tensor_tensor(acc[m, r][:], acc[m, r - 1][:], fetched[m][r][:], ADD)
 
         own_step(0)
-        own_step(1)
         shared_step(0, 0)
-        own_step(2)
+        own_step(1)
         shared_step(0, 1)
+        own_step(2)
+        shared_step(0, 2)
+        store(*shared[0], acc[0, 2])
+        shared_step(1, 0)
         own_step(3)
         store(1, 0, OWN, own[3])
-        shared_step(0, 2)
-        store(*shared[0], acc[0][2])
-        for r in range(3):
-            shared_step(1, r)
-        store(*shared[1], acc[1][2])
+        shared_step(1, 1)
+        shared_step(1, 2)
+        store(*shared[1], acc[1, 2])

from contextlib import ExitStack

import concourse.mybir as mybir

K, T, E, C, N = 1024, 512, 8, 256, 256
SLOTS = E * C
FLOPS = 2 * K * SLOTS * N
BYTES = 4 * K * T + E * K * N // 2 + E * K * N // 32 + 4 * SLOTS + 2 * 128 * 256 + 4 * N * T

F32 = mybir.dt.float32
BF16 = mybir.dt.bfloat16
I32 = mybir.dt.int32
U32 = mybir.dt.uint32
U16 = mybir.dt.uint16
U8 = mybir.dt.uint8
FP8X4 = mybir.dt.float8_e4m3fn_x4
FP4X4 = mybir.dt.float4_e2m1fn_x4
MULT = mybir.AluOpType.mult
ADD = mybir.AluOpType.add
COPY = mybir.ActivationFunctionType.Copy

P = 128
PACK = 4
PASSES = 2
HALVES = 2
RUN = 4
LIST_COLS = C // 16
PAIR = 2 * C
WINDOW = 2 * T
OWN = 128
EXTRA = 32
V_SLOTS = PAIR + EXTRA


def tile_moe_pre_lin_none_kernel(
    tc, xT, w_words, w_scales, gate, offs, pos1, pos2, pos3, pos4, out
):
    nc = tc.nc
    with ExitStack() as ctx:
        keep = ctx.enter_context(tc.tile_pool(name="keep", bufs=1))
        xb_pool = ctx.enter_context(tc.tile_pool(name="xb", bufs=3))
        psum = ctx.enter_context(tc.psum_pool(name="psum", bufs=1))

        x_sb = {}
        for a in range(PASSES):
            for t in range(PACK):
                x_sb[a, t] = keep.tile([P, WINDOW], F32, name="x%d%d" % (a, t))
                if (a, t) != (0, 0):
                    (nc.vector, nc.gpsimd)[a].memset(x_sb[a, t][:, T:WINDOW], 0.0)
        nc.scalar.activation(x_sb[0, 0][:, T:WINDOW], x_sb[0, 1][:, T:WINDOW], COPY)
        w_plane = keep.tile([P, E * PASSES, N], U8, align_bytes=64)
        nc.gpsimd.memset(w_plane[:].rearrange("p g n -> p (g n)").bitcast(I32), 0)

        offs_sb = keep.tile([P, SLOTS // 16], U16)
        nc.sync.dma_start(offs_sb[:], offs)
        x_rows = xT.rearrange("(a p t) w -> a t p w", a=PASSES, t=PACK)

        def load_x(a, t):
            nc.sync.dma_start(x_sb[a, t][:, 0:T], x_rows[a, t])

        def load_gate(name, s0, s1):
            tile = keep.tile([P, s1 - s0], F32, name=name, align_bytes=64)
            nc.sync.dma_start(tile[:], gate[0:P, s0:s1])
            return tile

        load_x(0, 0)
        gate_v = load_gate("gate_v", 0, V_SLOTS)
        for t in range(1, PACK):
            load_x(0, t)
        for t in range(PACK):
            load_x(1, t)
        gate_s = load_gate("gate_s", V_SLOTS, SLOTS)
        w_rows = w_words.rearrange("e a p b -> p (e a) b").bitcast(I32)
        w_sb = keep.tile([P, E * PASSES, 2 * N], U8, align_bytes=64)
        for g0 in range(0, E * PASSES, E):
            nc.sync.dma_start(w_sb[:, g0 : g0 + E, :].bitcast(I32), w_rows[:, g0 : g0 + E, :])
        scale_rows = w_scales.rearrange("e a (q r) n -> r q (e a) n", r=4).bitcast(I32)
        for r in range(4):
            nc.sync.dma_start(w_plane[r:P:32, :, :].bitcast(I32), scale_rows[r])
        pos_sb = []
        for r, pos in enumerate((pos1, pos2, pos3, pos4)):
            pos_sb.append(keep.tile([P, T // 16], U16, name="pos%d" % r))
            nc.sync.dma_start(pos_sb[r][:], pos)

        def slots_of(s0, s1, a, t):
            return x_sb[a, t][:].indirect(offs_sb[:, s0 // 16 : s1 // 16])

        def by_runs(planes):
            return planes.rearrange("p t (c i) -> p c t i", i=RUN)

        def woven(xb):
            return xb.rearrange("p (c i) t -> p c t i", i=RUN)

        codes = {}
        scales = {}

        def quantize(e, count, a, xb):
            words = keep.tile([P, count * C], U32, name="codes%d%d" % (e, a), align_bytes=64)
            plane = keep.tile([P, count * C], U8, name="scales%d%d" % (e, a), align_bytes=64)
            nc.vector.quantize_mx(
                out=words[:].bitcast(FP8X4),
                scales=plane[:],
                in_=xb[:].rearrange("p c t -> p (c t)"),
            )
            for m in range(count):
                codes[e + m, a] = words[:, m * C : (m + 1) * C]
                scales[e + m, a] = plane[:, m * C : (m + 1) * C]

        def s_gather(s0, s1, a, name):
            planes = keep.tile([P, PACK, s1 - s0], F32, name=name)
            for t in range(PACK):
                nc.scalar.activation(planes[:, t, :], slots_of(s0, s1, a, t), COPY)
            return planes

        v_planes = {}

        def v_gather(a, t):
            if t == 0:
                v_planes[a] = keep.tile([P, PACK, V_SLOTS], F32, name="v_planes%d" % a)
            nc.vector.tensor_tensor(v_planes[a][:, t, :], slots_of(0, V_SLOTS, a, t), gate_v[:], MULT)

        def weave(dst, planes):
            nc.vector.tensor_copy(woven(dst), by_runs(planes))

        def gate_weave(dst, planes, p0, s0, s1):
            g = gate_s[:, s0 - V_SLOTS : s1 - V_SLOTS].rearrange("p (c i) -> p c i", i=RUN)
            g = g.unsqueeze(2).to_broadcast([P, (s1 - s0) // RUN, PACK, RUN])
            nc.vector.tensor_tensor(woven(dst), by_runs(planes[:, :, s0 - p0 : s1 - p0]), g, MULT)

        def bf16_tile(width):
            return xb_pool.tile([P, width, PACK], BF16, name="xb", align_bytes=64)

        def one_pass(bank, e, h, a):
            g = e * PASSES + a
            nc.tensor.matmul_mx(
                out=bank,
                lhsT=w_sb[:, g, 2 * P * h : 2 * P * (h + 1)].bitcast(FP4X4),
                lhsT_scale=w_plane[:, g, P * h : P * (h + 1)],
                rhs=codes[e, a].bitcast(FP8X4),
                rhs_scale=scales[e, a],
                start=(a == 0),
                stop=(a == PASSES - 1),
            )

        banks = {}

        def multiply_pair(d):
            for h in range(HALVES):
                banks[d, h] = psum.tile([P, PAIR], F32, name="bank%d%d" % (d, h))
                for m in range(2):
                    for a in range(PASSES):
                        one_pass(banks[d, h][:, m * C : (m + 1) * C], 2 * d + m, h, a)


        def empty(d, h, copy):
            copy(y_sb[h][:, d * PAIR : (d + 1) * PAIR], banks[d, h][:])

        mid = [s_gather(V_SLOTS, 3 * PAIR, a, "mid%d" % a) for a in range(PASSES)]
        x1 = [keep.tile([P, PAIR, PACK], BF16, name="x1_%d" % a, align_bytes=64) for a in range(PASSES)]
        for t in range(PACK):
            v_gather(0, t)
        xz = bf16_tile(PAIR)
        weave(xz[:], v_planes[0][:, :, 0:PAIR])
        weave(x1[0][:, 0:EXTRA, :], v_planes[0][:, :, PAIR:V_SLOTS])
        end = [s_gather(3 * PAIR, SLOTS, 0, "v_planes0"), s_gather(3 * PAIR, SLOTS, 1, "end1")]
        v_gather(1, 0)
        quantize(0, 2, 0, xz)
        for t in range(1, PACK):
            v_gather(1, t)
        xb20 = keep.tile([P, PAIR, PACK], BF16, name="gate_v", align_bytes=64)
        gate_weave(xb20[:], mid[0], V_SLOTS, 2 * PAIR, 3 * PAIR)
        xz = bf16_tile(PAIR)
        weave(xz[:], v_planes[1][:, :, 0:PAIR])
        weave(x1[1][:, 0:EXTRA, :], v_planes[1][:, :, PAIR:V_SLOTS])
        quantize(4, 2, 0, xb20)
        gate_weave(x1[0][:, EXTRA:PAIR, :], mid[0], V_SLOTS, V_SLOTS, 2 * PAIR)
        quantize(0, 2, 1, xz)
        multiply_pair(0)
        gate_weave(x1[1][:, EXTRA:PAIR, :], mid[1], V_SLOTS, V_SLOTS, 2 * PAIR)
        quantize(2, 2, 0, x1[0])
        xb21 = bf16_tile(PAIR)
        gate_weave(xb21[:], mid[1], V_SLOTS, 2 * PAIR, 3 * PAIR)
        quantize(2, 2, 1, x1[1])
        multiply_pair(1)
        xb30 = bf16_tile(PAIR)
        gate_weave(xb30[:], end[0], 3 * PAIR, 3 * PAIR, SLOTS)
        quantize(4, 2, 1, xb21)
        multiply_pair(2)
        quantize(6, 2, 0, xb30)
        xb6 = bf16_tile(C)
        gate_weave(xb6[:], end[1], 3 * PAIR, 6 * C, 7 * C)
        xb7 = bf16_tile(C)
        gate_weave(xb7[:], end[1], 3 * PAIR, 7 * C, 8 * C)
        quantize(6, 1, 1, xb6)
        quantize(7, 1, 1, xb7)
        y_sb = [keep.tile([P, SLOTS], F32, name="y%d" % h) for h in range(HALVES)]
        for h in range(HALVES):
            empty(0, h, nc.scalar.copy)
        last = {}
        for h in range(HALVES):
            last[6, h] = psum.tile([P, C], F32, name="bank3%d" % h)
            last[7, h] = psum.tile([P, C], F32, name="bank0%d" % h)
        for a in range(PASSES):
            for e in (6, 7):
                for h in range(HALVES):
                    one_pass(last[e, h][:], e, h, a)
        empty(1, 0, nc.scalar.copy)
        empty(2, 0, nc.scalar.copy)
        empty(1, 1, nc.scalar.copy)
        empty(2, 1, nc.vector.tensor_copy)
        for e in (6, 7):
            nc.scalar.copy(y_sb[0][:, e * C : (e + 1) * C], last[e, 0][:])
            nc.vector.tensor_copy(y_sb[1][:, e * C : (e + 1) * C], last[e, 1][:])

        def picked(h, t0, t1, r):
            return y_sb[h][:].indirect(pos_sb[r][:, t0 // 16 : t1 // 16])

        def store(h, t0, t1, tile):
            nc.sync.dma_start(out[h * P : (h + 1) * P, t0:t1], tile[:])

        shared = [(0, 0, T), (1, OWN, T)]
        fetched = []
        for m, (h, t0, t1) in enumerate(shared):
            three = [keep.tile([P, t1 - t0], F32, name="f%d%d" % (m, r)) for r in range(3)]
            for r in range(3):
                nc.scalar.activation(three[r][:], picked(h, t0, t1, r), COPY)
            fetched.append(three)

        own = [keep.tile([P, OWN], F32, name="own%d" % r) for r in range(4)]
        acc = {}

        def own_step(r):
            if r == 0:
                nc.vector.tensor_copy(own[0][:], picked(1, 0, OWN, 0))
            else:
                nc.vector.tensor_tensor(own[r][:], picked(1, 0, OWN, r), own[r - 1][:], ADD)

        def shared_step(m, r):
            h, t0, t1 = shared[m]
            acc[m, r] = keep.tile([P, t1 - t0], F32, name="acc%d%d" % (m, r))
            if r == 0:
                nc.vector.tensor_tensor(acc[m, 0][:], picked(h, t0, t1, 3), fetched[m][0][:], ADD)
            else:
                nc.vector.tensor_tensor(acc[m, r][:], acc[m, r - 1][:], fetched[m][r][:], ADD)

        own_step(0)
        shared_step(0, 0)
        own_step(1)
        shared_step(0, 1)
        own_step(2)
        shared_step(0, 2)
        store(*shared[0], acc[0, 2])
        shared_step(1, 0)
        own_step(3)
        store(1, 0, OWN, own[3])
        shared_step(1, 1)
        shared_step(1, 2)
        store(*shared[1], acc[1, 2])
